import numpy as np
import ml_dtypes


def mxq(x, axis, fmt="e4m3"):
    dtype, down = {"e4m3": (ml_dtypes.float8_e4m3fn, 7), "e5m2": (ml_dtypes.float8_e5m2, 14)}[fmt]
    v = np.moveaxis(np.asarray(x, np.float32).astype(ml_dtypes.bfloat16).astype(np.float64), axis, -1)
    blocks = v.reshape(v.shape[:-1] + (-1, 32))
    amax = np.abs(blocks).max(-1, keepdims=True)
    byte = np.maximum(np.where(amax > 0, np.frexp(amax)[1] - 1 + 127, 0) - down, 1)
    scale = np.exp2(byte - 127.0)
    codes = (blocks / scale).astype(np.float32).astype(dtype).astype(np.float64)
    return np.moveaxis((codes * scale).reshape(v.shape), -1, axis)


WIDE = False


def mx_kscale(k):
    if not WIDE:
        return np.ones(k)
    levels = np.array([10, -10, 5, -5, 0])
    if k % 512:
        return np.exp2(np.random.permutation(np.resize(levels, k // 32))).repeat(32)
    a = np.empty((k // 512, 16))
    for p in range(k // 512):
        a[p, :8] = np.random.permutation(np.resize(levels, 8))
        for g in range(8):
            far = levels[np.abs(levels - a[p, g]) >= 10]
            a[p, g + 8] = far[np.random.randint(len(far))]
    return np.exp2(a.ravel()).repeat(32)


def f64(x):
    return np.asarray(x).astype(np.float64)


def striped(idx):
    return np.tile(np.asarray(idx).reshape(-1, 16).T, (8, 1)).astype(np.uint16)


def unstriped(offs):
    return offs[:16].T.reshape(-1).astype(np.int64)


E2M1 = np.array([0.0, 0.5, 1.0, 1.5, 2.0, 3.0, 4.0, 6.0, -0.0, -0.5, -1.0, -1.5, -2.0, -3.0, -4.0, -6.0])


def pack_weight(w, fmt):
    k, n = w.shape
    w = f64(np.asarray(w, np.float32).astype(ml_dtypes.bfloat16)).reshape(k // 32, 32, n)
    amax = np.abs(w).max(1)
    if fmt == "e4m3":
        byte = np.frexp(amax)[1] - 1 + 127 - 7
    else:
        mant, ex = np.frexp(amax / 6.0)
        byte = np.where(mant > 0.5, ex, ex - 1) + 127
    byte = np.clip(np.where(amax > 0, byte, 1), 1, 254)
    scaled = (w * np.exp2(127.0 - byte)[:, None, :]).reshape(k, n).astype(np.float32)
    by_word = np.ascontiguousarray(scaled.reshape(k // 512, 128, 4, n).transpose(0, 1, 3, 2))
    if fmt == "e4m3":
        words = by_word.astype(ml_dtypes.float8_e4m3fn).view(np.uint8)
    else:
        c = by_word.astype(ml_dtypes.float4_e2m1fn).view(np.uint8) & 0xF
        words = (c[..., 0::2] | (c[..., 1::2] << 4)).reshape(k // 512, 128, 2 * n)
    return np.ascontiguousarray(words), np.ascontiguousarray(byte.astype(np.uint8).reshape(k // 512, 16, n))


def unpack_weight(words, scales, fmt):
    g, _, n = scales.shape
    words = np.ascontiguousarray(words).reshape(g, 128, n, -1)
    if fmt == "e4m3":
        vals = words.view(ml_dtypes.float8_e4m3fn).astype(np.float64)
    else:
        nib = np.empty((g, 128, n, 4), np.uint8)
        nib[..., 0::2] = words & 0xF
        nib[..., 1::2] = words >> 4
        vals = E2M1[nib]
    vals = vals * np.repeat(np.exp2(scales.astype(np.float64) - 127.0), 8, axis=1)[..., None]
    return vals.transpose(0, 1, 3, 2).reshape(g * 512, n)


def bf(x):
    return np.asarray(x, np.float32).astype(ml_dtypes.bfloat16)


def planes(Y):
    r, m = Y.shape
    b = f64(bf(Y)).reshape(r // 32, 32, m)
    amax = np.abs(b).max(1)
    byte = np.clip(np.where(amax > 0, np.frexp(amax)[1] - 1 + 127 - 7, 1), 1, 254)
    codes = (b * np.exp2(127.0 - byte)[:, None, :]).reshape(r, m).astype(np.float32).astype(ml_dtypes.float8_e4m3fn).view(np.uint8)
    words = codes.reshape(r // 512, 128, 4, m).transpose(0, 1, 3, 2)
    return np.ascontiguousarray(words), np.ascontiguousarray(byte.astype(np.uint8).reshape(r // 512, 16, m))


K, T, J, R, N = 1024, 1024, 512, 512, 512


def setup_inputs():
    n = np.random.standard_normal
    idx = np.random.permutation(T)[:J]
    fk = mx_kscale(K)
    fr = mx_kscale(R)
    xtp = pack_weight(n((K, T)) / fk[:, None], "e2m1")
    wap = pack_weight(n((K, R)) * np.random.uniform(0.3, 2.0, (1, R)) / np.sqrt(K) * fk[:, None], "e4m3")
    wbp = pack_weight(n((R, N)) * 1 / np.sqrt(R) / fr[:, None], "e2m1")
    return {
        "xt_words": xtp[0],
        "xt_scales": xtp[1],
        "wa_words": wap[0],
        "wa_scales": wap[1],
        "us": (np.random.uniform(0.5, 2.0, (R, 1)) * fr[:, None]).astype(np.float32),
        "wb_words": wbp[0],
        "wb_scales": wbp[1],
        "res": (1.0 * n((N, T))).astype(np.float32),
        "offs": striped(idx),
    }


def reference(xt_words, xt_scales, wa_words, wa_scales, us, wb_words, wb_scales, res, offs):
    idx = unstriped(offs)
    xtu = unpack_weight(xt_words, xt_scales, "e2m1")
    wau = unpack_weight(wa_words, wa_scales, "e4m3")
    wbu = unpack_weight(wb_words, wb_scales, "e2m1")
    xtidxg = xtu[:, idx]
    z = wau.T @ xtidxg
    hid = z / (np.max(np.abs(z), axis=1, keepdims=True) + 0.1) * f64(us)
    hidq = mxq(hid, 0, "e4m3")
    p = wbu.T @ hidq
    pp = np.zeros((N, T))
    pp[:, idx] = p
    y = pp + 0.2 * f64(res)
    words, scales = planes(y)
    return y, words, scales

@@ -1,0 +1,205 @@
+from contextlib import ExitStack
+
+import concourse.mybir as mybir
+
+K, T, J, R, N = 1024, 1024, 512, 512, 512
+FLOPS = 2 * K * R * J + 2 * R * N * J
+
+F32 = mybir.dt.float32
+BF16 = mybir.dt.bfloat16
+I32 = mybir.dt.int32
+U32 = mybir.dt.uint32
+U16 = mybir.dt.uint16
+U8 = mybir.dt.uint8
+FP8X4 = mybir.dt.float8_e4m3fn_x4
+FP4X4 = mybir.dt.float4_e2m1fn_x4
+ALU = mybir.AluOpType
+ACT = mybir.ActivationFunctionType
+AXIS = mybir.AxisListType
+
+P = 128
+PACK = 4
+PASSES = K // (P * PACK)
+HALF = J // 2
+BLOCK = 128
+COLS = T // 2
+
+
+def deal(nc, dst, src, run):
+    nc.vector.tensor_copy(
+        out=dst.rearrange("p g (t b i) -> p g b t i", t=PACK, i=run),
+        in_=src.rearrange("p g (b i t) -> p g b t i", t=PACK, i=run),
+    )
+
+
+def load_scale_rows(nc, plane, scales):
+    rows = scales.rearrange("g (Q q) c -> q Q g c", q=4)
+    for q in range(4):
+        nc.scalar.dma_start(out=plane[q:P:32].bitcast(I32), in_=rows[q].bitcast(I32))
+
+
+def tile_moe_expert_hidden_over_peak_pl_kernel(
+    tc, xt_words, xt_scales, wa_words, wa_scales, us, wb_words, wb_scales, res, offs, out_0, out_1, out_2
+):
+    nc = tc.nc
+    with ExitStack() as ctx:
+        keep = ctx.enter_context(tc.tile_pool(name="keep", bufs=1))
+        psum = ctx.enter_context(tc.psum_pool(name="psum", bufs=1))
+
+        offsets = keep.tile([P, J // 16], U16, name="offsets")
+        nc.sync.dma_start(offsets[:], offs)
+
+        x_scale = keep.tile([P, PASSES, T], U8, name="x_scale", align_bytes=64)
+        wa_scale_raw = keep.tile([P, PASSES, R], U8, name="wa_scale_raw", tag="early", align_bytes=64)
+        wb_scale_raw = keep.tile([P, 1, N], U8, name="wb_scale_raw", align_bytes=64)
+        for plane in (wa_scale_raw, x_scale, wb_scale_raw):
+            nc.vector.memset(plane[:].bitcast(I32), 0)
+
+        x_word = [keep.tile([P, 2 * T], U8, name=f"x_word{g}", align_bytes=64) for g in range(PASSES)]
+        for g in range(PASSES):
+            nc.sync.dma_start(out=x_word[g][:].bitcast(I32), in_=xt_words[g].bitcast(I32))
+        wa_raw = keep.tile([P, PASSES, R], I32, name="wa_raw", tag="staged", align_bytes=64)
+        nc.sync.dma_start(out=wa_raw[:], in_=wa_words.rearrange("g p c r -> p g (c r)").bitcast(I32))
+        load_scale_rows(nc, wa_scale_raw, wa_scales)
+        load_scale_rows(nc, x_scale, xt_scales)
+        load_scale_rows(nc, wb_scale_raw, wb_scales)
+        factor = keep.tile([P, PACK], F32, name="factor")
+        nc.gpsimd.dma_start(out=factor[:], in_=us.rearrange("(p t) o -> p (t o)", t=PACK))
+
+        placed = [keep.tile([P, T], F32, name=f"placed{t}") for t in range(PACK)]
+        for t in range(PACK):
+            nc.vector.memset(placed[t][:], 0.0)
+
+        lists = [offsets[:, h * (HALF // 16) : (h + 1) * (HALF // 16)] for h in range(2)]
+        g_word = [[keep.tile([P, 2 * HALF], U8, name=f"g_word{h}{g}", align_bytes=64) for g in range(PASSES)] for h in range(2)]
+        g_scale = [[keep.tile([P, HALF], U8, name=f"g_scale{h}{g}", align_bytes=64) for g in range(PASSES)] for h in range(2)]
+
+        def gather_words(h):
+            for g in range(PASSES):
+                nc.vector.tensor_copy(g_word[h][g][:].bitcast(U16), x_word[g][:].bitcast(U16).indirect(lists[h]))
+
+        def gather_scales(h):
+            for g in range(PASSES):
+                nc.vector.tensor_copy(g_scale[h][g][:], x_scale[:, g, :].indirect(lists[h]))
+
+        wa_word = keep.tile([P, PASSES, R], I32, name="wa_word", align_bytes=64)
+        wa_scale = keep.tile([P, PASSES, R], U8, name="wa_scale", align_bytes=64)
+        gather_words(0)
+        deal(nc, wa_word[:], wa_raw[:], 4)
+        deal(nc, wa_scale[:], wa_scale_raw[:], 16)
+        gather_scales(0)
+        gather_words(1)
+        gather_scales(1)
+
+        wb_raw = keep.tile([P, 1, 2 * N], U8, name="wb_raw", tag="early", align_bytes=64)
+        nc.sync.dma_start(out=wb_raw[:].bitcast(I32), in_=wb_words.rearrange("g p c -> p g c").bitcast(I32))
+        stream = keep.tile([P, PACK, T], F32, name="stream", tag="staged", align_bytes=64)
+        nc.sync.dma_start(out=stream[:], in_=res.rearrange("(p t) c -> p t c", t=PACK))
+
+        z = [psum.tile([P, PACK, BLOCK], F32, name=f"z{b}") for b in range(4)]
+        for b in range(4):
+            h, c = divmod(b, 2)
+            for t in range(PACK):
+                for g in range(PASSES):
+                    nc.tensor.matmul_mx(
+                        out=z[b][:, t, :],
+                        lhsT=wa_word[:, g, t * P : (t + 1) * P].bitcast(FP8X4),
+                        lhsT_scale=wa_scale[:, g, t * P : (t + 1) * P],
+                        rhs=g_word[h][g][:, 2 * c * BLOCK : 2 * (c + 1) * BLOCK].bitcast(FP4X4),
+                        rhs_scale=g_scale[h][g][:, c * BLOCK : (c + 1) * BLOCK],
+                        start=(g == 0),
+                        stop=(g == PASSES - 1),
+                    )
+
+        size_a = keep.tile([P, PACK, HALF], F32, name="size_a")
+        size_b = keep.tile([P, PACK, BLOCK], F32, name="size_b")
+        size_c = keep.tile([P, PACK, BLOCK + 8], F32, name="size_c")
+        nc.scalar.activation(size_a[:, :, 0:BLOCK], z[0][:], ACT.Abs)
+        nc.scalar.activation(size_a[:, :, BLOCK:HALF], z[1][:], ACT.Abs)
+        nc.scalar.activation(size_b[:], z[2][:], ACT.Abs)
+        nc.scalar.activation(size_c[:, :, 0:BLOCK], z[3][:], ACT.Abs)
+        nc.vector.tensor_reduce(size_c[:, :, BLOCK], size_a[:], AXIS.X, ALU.max)
+
+        wb_word = keep.tile([P, 1, 2 * N], U8, name="wb_word", align_bytes=64)
+        wb_scale = keep.tile([P, 1, N], U8, name="wb_scale", align_bytes=64)
+        deal(nc, wb_word[:].bitcast(U16), wb_raw[:].bitcast(U16), 8)
+        deal(nc, wb_scale[:], wb_scale_raw[:], 16)
+
+        nc.vector.tensor_reduce(size_c[:, :, BLOCK + 1], size_b[:], AXIS.X, ALU.max)
+        peak = keep.tile([P, PACK], F32, name="peak")
+        nc.vector.tensor_reduce(peak[:], size_c[:, :, 0 : BLOCK + 2], AXIS.X, ALU.max)
+        divisor = keep.tile([P, PACK], F32, name="divisor")
+        nc.vector.tensor_scalar(divisor[:], peak[:], 0.1, None, ALU.add)
+        inverse = keep.tile([P, PACK], F32, name="inverse")
+        nc.vector.reciprocal(inverse[:], divisor[:])
+        gain = keep.tile([P, PACK], F32, name="gain")
+        nc.vector.tensor_tensor(gain[:], inverse[:], factor[:], ALU.mult)
+
+        hid = [keep.tile([P, HALF, PACK], BF16, name=f"hid{h}", align_bytes=64) for h in range(2)]
+        h_word = [keep.tile([P, HALF], U32, name=f"h_word{h}", align_bytes=64) for h in range(2)]
+        h_scale = [keep.tile([P, HALF], U8, name=f"h_scale{h}", align_bytes=64) for h in range(2)]
+        p_bank = [psum.tile([P, J], F32, name=f"p_bank{t}") for t in range(PACK)]
+        p_sb = [keep.tile([P, J], F32, name=f"p_sb{t}") for t in range(PACK)]
+        for h in range(2):
+            for c in range(2):
+                nc.vector.tensor_tensor(
+                    hid[h][:, c * BLOCK : (c + 1) * BLOCK, :],
+                    z[2 * h + c][:].rearrange("p t j -> p j t"),
+                    gain[:].unsqueeze(1).to_broadcast([P, BLOCK, PACK]),
+                    ALU.mult,
+                )
+            nc.vector.quantize_mx(
+                out=h_word[h][:].bitcast(FP8X4), scales=h_scale[h][:], in_=hid[h][:].rearrange("p j t -> p (j t)")
+            )
+            cols = slice(h * HALF, (h + 1) * HALF)
+            for t in range(PACK):
+                nc.tensor.matmul_mx(
+                    out=p_bank[t][:, cols],
+                    lhsT=wb_word[:, 0, 2 * t * P : 2 * (t + 1) * P].bitcast(FP4X4),
+                    lhsT_scale=wb_scale[:, 0, t * P : (t + 1) * P],
+                    rhs=h_word[h][:].bitcast(FP8X4),
+                    rhs_scale=h_scale[h][:],
+                    start=True,
+                    stop=True,
+                )
+                nc.scalar.copy(p_sb[t][:, cols], p_bank[t][:, cols])
+
+        y = [[keep.tile([P, 2, COLS], F32, name=f"y{u}{k}") for k in range(2)] for u in range(2)]
+        y_round = [keep.tile([P, COLS, PACK], BF16, name=f"y_round{k}", align_bytes=64) for k in range(2)]
+        y_word = [keep.tile([P, COLS], U32, name=f"y_word{k}", align_bytes=64) for k in range(2)]
+        y_scale = keep.tile([P, T], U8, name="y_scale", align_bytes=64)
+        out_rows = out_0.rearrange("(p t) c -> p t c", t=PACK)
+        out_words = out_1[0].rearrange("p c r -> p (c r)").bitcast(I32)
+
+        def add_stream(t, k):
+            u, e = divmod(t, 2)
+            cols = slice(k * COLS, (k + 1) * COLS)
+            nc.vector.scalar_tensor_tensor(y[u][k][:, e, :], stream[:, t, cols], 0.2, placed[t][:, cols], ALU.mult, ALU.add)
+            nc.sync.dma_start(out=out_rows[:, t, cols], in_=y[u][k][:, e, :])
+
+        def round_pair(copy, u, k, cols):
+            copy(y_round[k][:, cols, 2 * u : 2 * u + 2], y[u][k][:, :, cols].rearrange("p e c -> p c e"))
+
+        for t in range(PACK):
+            if t == 0:
+                for h in range(2):
+                    nc.vector.tensor_copy(placed[t][:].indirect(lists[h]), p_sb[t][:, h * HALF : (h + 1) * HALF])
+            else:
+                nc.vector.tensor_copy(placed[t][:].indirect(offsets[:]), p_sb[t][:])
+            for k in range(2):
+                add_stream(t, k)
+                if t == 1:
+                    round_pair(nc.scalar.copy, 0, k, slice(0, COLS))
+        for k in range(2):
+            round_pair(nc.scalar.copy, 1, k, slice(0, COLS // 2))
+        for k in range(2):
+            round_pair(nc.vector.tensor_copy, 1, k, slice(COLS // 2, COLS))
+            nc.vector.quantize_mx(
+                out=y_word[k][:].bitcast(FP8X4),
+                scales=y_scale[:, k * COLS : (k + 1) * COLS],
+                in_=y_round[k][:].rearrange("p c t -> p (c t)"),
+            )
+            nc.sync.dma_start(out=out_words[:, k * COLS : (k + 1) * COLS], in_=y_word[k][:].bitcast(I32))
+        out_scale_rows = out_2[0].rearrange("(Q q) c -> q Q c", q=4)
+        for q in range(4):
+            nc.scalar.dma_start(out=out_scale_rows[q].bitcast(I32), in_=y_scale[q:P:32].bitcast(I32))

@@ -66,9 +66,10 @@ def tile_moe_expert_hidden_over_peak_pl_kernel(
         factor = keep.tile([P, PACK], F32, name="factor")
         nc.gpsimd.dma_start(out=factor[:], in_=us.rearrange("(p t) o -> p (t o)", t=PACK))
 
-        placed = [keep.tile([P, T], F32, name=f"placed{t}") for t in range(PACK)]
-        for t in range(PACK):
-            nc.vector.memset(placed[t][:], 0.0)
+        windows = [keep.tile([P, T], F32, name=f"window{w}") for w in range(2)]
+        for w in range(2):
+            nc.vector.memset(windows[w][:], 0.0)
+        placed = [windows[t % 2] for t in range(PACK)]
 
         lists = [offsets[:, h * (HALF // 16) : (h + 1) * (HALF // 16)] for h in range(2)]
         g_word = [[keep.tile([P, 2 * HALF], U8, name=f"g_word{h}{g}", align_bytes=64) for g in range(PASSES)] for h in range(2)]
@@ -113,7 +114,7 @@ def tile_moe_expert_hidden_over_peak_pl_kernel(
 
         size_a = keep.tile([P, PACK, HALF], F32, name="size_a")
         size_b = keep.tile([P, PACK, BLOCK], F32, name="size_b")
-        size_c = keep.tile([P, PACK, BLOCK + 8], F32, name="size_c")
+        size_c = keep.tile([P, PACK, BLOCK + 8], F32, name="size_c", tag="after_peak")
         nc.scalar.activation(size_a[:, :, 0:BLOCK], z[0][:], ACT.Abs)
         nc.scalar.activation(size_a[:, :, BLOCK:HALF], z[1][:], ACT.Abs)
         nc.scalar.activation(size_b[:], z[2][:], ACT.Abs)
@@ -139,7 +140,10 @@ def tile_moe_expert_hidden_over_peak_pl_kernel(
         h_word = [keep.tile([P, HALF], U32, name=f"h_word{h}", align_bytes=64) for h in range(2)]
         h_scale = [keep.tile([P, HALF], U8, name=f"h_scale{h}", align_bytes=64) for h in range(2)]
         p_bank = [psum.tile([P, J], F32, name=f"p_bank{t}") for t in range(PACK)]
-        p_sb = [keep.tile([P, J], F32, name=f"p_sb{t}") for t in range(PACK)]
+        p_sb = [keep.tile([P, J], F32, name=f"p_sb{t}", tag=f"p_sb{t}") for t in range(PACK)]
+        fifth_a = keep.tile([P, 2, T], F32, name="fifth_a", tag="after_peak")
+        nc.scalar.mul(fifth_a[:], stream[:, 0:2, :], 0.2)
+        fifth = [fifth_a[:, 0, :], fifth_a[:, 1, :]]
         for h in range(2):
             for c in range(2):
                 nc.vector.tensor_tensor(
@@ -174,7 +178,10 @@ def tile_moe_expert_hidden_over_peak_pl_kernel(
         def add_stream(t, k):
             u, e = divmod(t, 2)
             cols = slice(k * COLS, (k + 1) * COLS)
-            nc.vector.scalar_tensor_tensor(y[u][k][:, e, :], stream[:, t, cols], 0.2, placed[t][:, cols], ALU.mult, ALU.add)
+            if t < PACK - 1:
+                nc.gpsimd.tensor_tensor(y[u][k][:, e, :], fifth[t][:, cols], placed[t][:, cols], ALU.add)
+            else:
+                nc.vector.scalar_tensor_tensor(y[u][k][:, e, :], stream[:, t, cols], 0.2, placed[t][:, cols], ALU.mult, ALU.add)
             nc.sync.dma_start(out=out_rows[:, t, cols], in_=y[u][k][:, e, :])
 
         def round_pair(copy, u, k, cols):
@@ -184,6 +191,9 @@ def tile_moe_expert_hidden_over_peak_pl_kernel(
             if t == 0:
                 for h in range(2):
                     nc.vector.tensor_copy(placed[t][:].indirect(lists[h]), p_sb[t][:, h * HALF : (h + 1) * HALF])
+                fifth_b = keep.tile([P, T], F32, name="fifth_b", tag="p_sb0")
+                nc.scalar.mul(fifth_b[:], stream[:, 2, :], 0.2)
+                fifth.append(fifth_b[:])
             else:
                 nc.vector.tensor_copy(placed[t][:].indirect(offsets[:]), p_sb[t][:])
             for k in range(2):

@@ -32,10 +32,10 @@ def deal(nc, dst, src, run):
     )
 
 
-def load_scale_rows(nc, plane, scales):
+def load_scale_rows(queue, plane, scales):
     rows = scales.rearrange("g (Q q) c -> q Q g c", q=4)
     for q in range(4):
-        nc.scalar.dma_start(out=plane[q:P:32].bitcast(I32), in_=rows[q].bitcast(I32))
+        queue.dma_start(out=plane[q:P:32].bitcast(I32), in_=rows[q].bitcast(I32))
 
 
 def tile_moe_expert_hidden_over_peak_pl_kernel(
@@ -44,31 +44,32 @@ def tile_moe_expert_hidden_over_peak_pl_kernel(
     nc = tc.nc
     with ExitStack() as ctx:
         keep = ctx.enter_context(tc.tile_pool(name="keep", bufs=1))
+        reuse = ctx.enter_context(tc.tile_pool(name="reuse", bufs=1))
         psum = ctx.enter_context(tc.psum_pool(name="psum", bufs=1))
 
         offsets = keep.tile([P, J // 16], U16, name="offsets")
         nc.sync.dma_start(offsets[:], offs)
 
         x_scale = keep.tile([P, PASSES, T], U8, name="x_scale", align_bytes=64)
-        wa_scale_raw = keep.tile([P, PASSES, R], U8, name="wa_scale_raw", tag="early", align_bytes=64)
+        wa_scale_raw = keep.tile([P, PASSES, R], U8, name="wa_scale_raw", align_bytes=64)
         wb_scale_raw = keep.tile([P, 1, N], U8, name="wb_scale_raw", align_bytes=64)
         for plane in (wa_scale_raw, x_scale, wb_scale_raw):
-            nc.vector.memset(plane[:].bitcast(I32), 0)
+            nc.gpsimd.memset(plane[:].bitcast(I32), 0)
 
-        x_word = [keep.tile([P, 2 * T], U8, name=f"x_word{g}", align_bytes=64) for g in range(PASSES)]
+        x_word = [keep.tile([P, 2 * T], U8, name=f"x_word{g}", tag=f"x_word{g}", align_bytes=64) for g in range(PASSES)]
         for g in range(PASSES):
             nc.sync.dma_start(out=x_word[g][:].bitcast(I32), in_=xt_words[g].bitcast(I32))
-        wa_raw = keep.tile([P, PASSES, R], I32, name="wa_raw", tag="staged", align_bytes=64)
+        wa_raw = reuse.tile([P, PASSES, R], I32, name="wa_raw", offset=0)
         nc.sync.dma_start(out=wa_raw[:], in_=wa_words.rearrange("g p c r -> p g (c r)").bitcast(I32))
-        load_scale_rows(nc, wa_scale_raw, wa_scales)
-        load_scale_rows(nc, x_scale, xt_scales)
-        load_scale_rows(nc, wb_scale_raw, wb_scales)
-        factor = keep.tile([P, PACK], F32, name="factor")
-        nc.gpsimd.dma_start(out=factor[:], in_=us.rearrange("(p t) o -> p (t o)", t=PACK))
+        load_scale_rows(nc.scalar, wa_scale_raw, wa_scales)
+        load_scale_rows(nc.sync, x_scale, xt_scales)
+        load_scale_rows(nc.sync, wb_scale_raw, wb_scales)
 
         windows = [keep.tile([P, T], F32, name=f"window{w}") for w in range(2)]
         for w in range(2):
-            nc.vector.memset(windows[w][:], 0.0)
+            nc.gpsimd.memset(windows[w][:], 0.0)
+        warm = keep.tile([P, 1], F32, name="warm")
+        nc.scalar.activation(warm[:], windows[0][:, 0:1], ACT.Abs)
         placed = [windows[t % 2] for t in range(PACK)]
 
         lists = [offsets[:, h * (HALF // 16) : (h + 1) * (HALF // 16)] for h in range(2)]
@@ -92,9 +93,11 @@ def tile_moe_expert_hidden_over_peak_pl_kernel(
         gather_words(1)
         gather_scales(1)
 
-        wb_raw = keep.tile([P, 1, 2 * N], U8, name="wb_raw", tag="early", align_bytes=64)
+        wb_raw = reuse.tile([P, 1, 2 * N], U8, name="wb_raw", offset=0)
         nc.sync.dma_start(out=wb_raw[:].bitcast(I32), in_=wb_words.rearrange("g p c -> p g c").bitcast(I32))
-        stream = keep.tile([P, PACK, T], F32, name="stream", tag="staged", align_bytes=64)
+        factor = reuse.tile([P, PACK], F32, name="factor", offset=3 * N)
+        nc.sync.dma_start(out=factor[:], in_=us.rearrange("(p t) o -> p (t o)", t=PACK))
+        stream = keep.tile([P, PACK, T], F32, name="stream", tag="x_word0", align_bytes=64)
         nc.sync.dma_start(out=stream[:], in_=res.rearrange("(p t) c -> p t c", t=PACK))
 
         z = [psum.tile([P, PACK, BLOCK], F32, name=f"z{b}") for b in range(4)]
@@ -112,53 +115,61 @@ def tile_moe_expert_hidden_over_peak_pl_kernel(
                         stop=(g == PASSES - 1),
                     )
 
-        size_a = keep.tile([P, PACK, HALF], F32, name="size_a")
-        size_b = keep.tile([P, PACK, BLOCK], F32, name="size_b")
-        size_c = keep.tile([P, PACK, BLOCK + 8], F32, name="size_c", tag="after_peak")
-        nc.scalar.activation(size_a[:, :, 0:BLOCK], z[0][:], ACT.Abs)
-        nc.scalar.activation(size_a[:, :, BLOCK:HALF], z[1][:], ACT.Abs)
-        nc.scalar.activation(size_b[:], z[2][:], ACT.Abs)
-        nc.scalar.activation(size_c[:, :, 0:BLOCK], z[3][:], ACT.Abs)
-        nc.vector.tensor_reduce(size_c[:, :, BLOCK], size_a[:], AXIS.X, ALU.max)
+        widths = (HALF, BLOCK, BLOCK)
+        size = [keep.tile([P, PACK, w], F32, name=f"size{i}", tag=f"size{i}", align_bytes=64) for i, w in enumerate(widths)]
+        for c in range(2):
+            nc.scalar.activation(size[0][:, :, c * BLOCK : (c + 1) * BLOCK], z[c][:], ACT.Abs)
+        for i in (1, 2):
+            nc.scalar.activation(size[i][:], z[i + 1][:], ACT.Abs)
+        z_last = keep.tile([P, BLOCK, PACK], F32, name="z_last")
+        nc.scalar.copy(z_last[:], z[3][:].rearrange("p t j -> p j t"))
 
-        wb_word = keep.tile([P, 1, 2 * N], U8, name="wb_word", align_bytes=64)
-        wb_scale = keep.tile([P, 1, N], U8, name="wb_scale", align_bytes=64)
+        divisor = None
+        for i in range(3):
+            peak = keep.tile([P, PACK], F32, name=f"peak{i}", tag=f"peak{i}", align_bytes=64)
+            nc.vector.tensor_reduce(peak[:], size[i][:], AXIS.X, ALU.max)
+            running = keep.tile([P, PACK], F32, name=f"running{i}", tag=f"running{i}", align_bytes=64)
+            if i == 0:
+                nc.vector.tensor_scalar(running[:], peak[:], 0.1, None, ALU.add)
+            else:
+                nc.vector.scalar_tensor_tensor(running[:], peak[:], 0.1, divisor[:], ALU.add, ALU.max)
+            divisor = running
+        wb_word = keep.tile([P, 1, 2 * N], U8, name="wb_word", tag="size2", align_bytes=64)
         deal(nc, wb_word[:].bitcast(U16), wb_raw[:].bitcast(U16), 8)
-        deal(nc, wb_scale[:], wb_scale_raw[:], 16)
-
-        nc.vector.tensor_reduce(size_c[:, :, BLOCK + 1], size_b[:], AXIS.X, ALU.max)
-        peak = keep.tile([P, PACK], F32, name="peak")
-        nc.vector.tensor_reduce(peak[:], size_c[:, :, 0 : BLOCK + 2], AXIS.X, ALU.max)
-        divisor = keep.tile([P, PACK], F32, name="divisor")
-        nc.vector.tensor_scalar(divisor[:], peak[:], 0.1, None, ALU.add)
         inverse = keep.tile([P, PACK], F32, name="inverse")
         nc.vector.reciprocal(inverse[:], divisor[:])
+        wb_scale = keep.tile([P, 1, N], U8, name="wb_scale", tag="running2", align_bytes=64)
+        deal(nc, wb_scale[:], wb_scale_raw[:], 16)
         gain = keep.tile([P, PACK], F32, name="gain")
         nc.vector.tensor_tensor(gain[:], inverse[:], factor[:], ALU.mult)
 
         hid = [keep.tile([P, HALF, PACK], BF16, name=f"hid{h}", align_bytes=64) for h in range(2)]
-        h_word = [keep.tile([P, HALF], U32, name=f"h_word{h}", align_bytes=64) for h in range(2)]
+        h_word = [keep.tile([P, HALF], U32, name=f"h_word{h}", tag=f"h_word{h}", align_bytes=64) for h in range(2)]
         h_scale = [keep.tile([P, HALF], U8, name=f"h_scale{h}", align_bytes=64) for h in range(2)]
-        p_bank = [psum.tile([P, J], F32, name=f"p_bank{t}") for t in range(PACK)]
-        p_sb = [keep.tile([P, J], F32, name=f"p_sb{t}", tag=f"p_sb{t}") for t in range(PACK)]
-        fifth_a = keep.tile([P, 2, T], F32, name="fifth_a", tag="after_peak")
-        nc.scalar.mul(fifth_a[:], stream[:, 0:2, :], 0.2)
-        fifth = [fifth_a[:, 0, :], fifth_a[:, 1, :]]
+        p_bank = [[psum.tile([P, 2, HALF], F32, name=f"p_bank{h}{u}") for u in range(2)] for h in range(2)]
+        p_sb = [keep.tile([P, J], F32, name=f"p_sb{t}") for t in range(PACK)]
+        fifth = []
+
+        def scale_stream(t, tag, align):
+            part = keep.tile([P, T], F32, name=f"fifth{t}", tag=tag, align_bytes=align)
+            nc.scalar.mul(part[:], stream[:, t, :], 0.2)
+            fifth.append(part[:])
+
+        scale_stream(0, "size1", 64)
+        scale_stream(1, "peak2", 64)
+        spread = gain[:].unsqueeze(1).to_broadcast([P, BLOCK, PACK])
+        nc.gpsimd.tensor_tensor(hid[1][:, BLOCK:HALF, :], z_last[:], spread, ALU.mult)
+        for b in range(3):
+            h, c = divmod(b, 2)
+            nc.vector.tensor_tensor(hid[h][:, c * BLOCK : (c + 1) * BLOCK, :], z[b][:].rearrange("p t j -> p j t"), spread, ALU.mult)
         for h in range(2):
-            for c in range(2):
-                nc.vector.tensor_tensor(
-                    hid[h][:, c * BLOCK : (c + 1) * BLOCK, :],
-                    z[2 * h + c][:].rearrange("p t j -> p j t"),
-                    gain[:].unsqueeze(1).to_broadcast([P, BLOCK, PACK]),
-                    ALU.mult,
-                )
             nc.vector.quantize_mx(
                 out=h_word[h][:].bitcast(FP8X4), scales=h_scale[h][:], in_=hid[h][:].rearrange("p j t -> p (j t)")
             )
             cols = slice(h * HALF, (h + 1) * HALF)
             for t in range(PACK):
                 nc.tensor.matmul_mx(
-                    out=p_bank[t][:, cols],
+                    out=p_bank[h][t // 2][:, t % 2, :],
                     lhsT=wb_word[:, 0, 2 * t * P : 2 * (t + 1) * P].bitcast(FP4X4),
                     lhsT_scale=wb_scale[:, 0, t * P : (t + 1) * P],
                     rhs=h_word[h][:].bitcast(FP8X4),
@@ -166,7 +177,12 @@ def tile_moe_expert_hidden_over_peak_pl_kernel(
                     start=True,
                     stop=True,
                 )
-                nc.scalar.copy(p_sb[t][:, cols], p_bank[t][:, cols])
+            for t in range(2):
+                nc.scalar.copy(p_sb[t][:, cols], p_bank[h][0][:, t, :])
+        for h in range(2):
+            for t in range(2, PACK):
+                nc.scalar.copy(p_sb[t][:, h * HALF : (h + 1) * HALF], p_bank[h][1][:, t % 2, :])
+        scale_stream(2, "h_word1", 64)
 
         y = [[keep.tile([P, 2, COLS], F32, name=f"y{u}{k}") for k in range(2)] for u in range(2)]
         y_round = [keep.tile([P, COLS, PACK], BF16, name=f"y_round{k}", align_bytes=64) for k in range(2)]
@@ -191,9 +207,6 @@ def tile_moe_expert_hidden_over_peak_pl_kernel(
             if t == 0:
                 for h in range(2):
                     nc.vector.tensor_copy(placed[t][:].indirect(lists[h]), p_sb[t][:, h * HALF : (h + 1) * HALF])
-                fifth_b = keep.tile([P, T], F32, name="fifth_b", tag="p_sb0")
-                nc.scalar.mul(fifth_b[:], stream[:, 2, :], 0.2)
-                fifth.append(fifth_b[:])
             else:
                 nc.vector.tensor_copy(placed[t][:].indirect(offsets[:]), p_sb[t][:])
             for k in range(2):
@@ -204,6 +217,7 @@ def tile_moe_expert_hidden_over_peak_pl_kernel(
             round_pair(nc.scalar.copy, 1, k, slice(0, COLS // 2))
         for k in range(2):
             round_pair(nc.vector.tensor_copy, 1, k, slice(COLS // 2, COLS))
+        for k in range(2):
             nc.vector.quantize_mx(
                 out=y_word[k][:].bitcast(FP8X4),
                 scales=y_scale[:, k * COLS : (k + 1) * COLS],
@@ -212,4 +226,5 @@ def tile_moe_expert_hidden_over_peak_pl_kernel(
             nc.sync.dma_start(out=out_words[:, k * COLS : (k + 1) * COLS], in_=y_word[k][:].bitcast(I32))
         out_scale_rows = out_2[0].rearrange("(Q q) c -> q Q c", q=4)
         for q in range(4):
-            nc.scalar.dma_start(out=out_scale_rows[q].bitcast(I32), in_=y_scale[q:P:32].bitcast(I32))
+            queue = nc.scalar if q < 2 else nc.sync
+            queue.dma_start(out=out_scale_rows[q].bitcast(I32), in_=y_scale[q:P:32].bitcast(I32))

@@ -51,30 +51,37 @@ def tile_moe_expert_hidden_over_peak_pl_kernel(
         nc.sync.dma_start(offsets[:], offs)
 
         x_scale = keep.tile([P, PASSES, T], U8, name="x_scale", align_bytes=64)
-        wa_scale_raw = keep.tile([P, PASSES, R], U8, name="wa_scale_raw", align_bytes=64)
+        wa_scale_raw = reuse.tile([P, PASSES, R], U8, name="wa_scale_raw", offset=8 * R)
         wb_scale_raw = keep.tile([P, 1, N], U8, name="wb_scale_raw", align_bytes=64)
-        for plane in (wa_scale_raw, x_scale, wb_scale_raw):
-            nc.gpsimd.memset(plane[:].bitcast(I32), 0)
+        for plane in (x_scale, wa_scale_raw, wb_scale_raw):
+            nc.vector.memset(plane[:].bitcast(I32), 0)
 
         x_word = [keep.tile([P, 2 * T], U8, name=f"x_word{g}", tag=f"x_word{g}", align_bytes=64) for g in range(PASSES)]
         for g in range(PASSES):
             nc.sync.dma_start(out=x_word[g][:].bitcast(I32), in_=xt_words[g].bitcast(I32))
         wa_raw = reuse.tile([P, PASSES, R], I32, name="wa_raw", offset=0)
         nc.sync.dma_start(out=wa_raw[:], in_=wa_words.rearrange("g p c r -> p g (c r)").bitcast(I32))
-        load_scale_rows(nc.scalar, wa_scale_raw, wa_scales)
-        load_scale_rows(nc.sync, x_scale, xt_scales)
+        load_scale_rows(nc.scalar, x_scale, xt_scales)
+        load_scale_rows(nc.sync, wa_scale_raw, wa_scales)
         load_scale_rows(nc.sync, wb_scale_raw, wb_scales)
 
         windows = [keep.tile([P, T], F32, name=f"window{w}") for w in range(2)]
         for w in range(2):
-            nc.gpsimd.memset(windows[w][:], 0.0)
-        warm = keep.tile([P, 1], F32, name="warm")
-        nc.scalar.activation(warm[:], windows[0][:, 0:1], ACT.Abs)
+            nc.vector.memset(windows[w][:], 0.0)
         placed = [windows[t % 2] for t in range(PACK)]
 
         lists = [offsets[:, h * (HALF // 16) : (h + 1) * (HALF // 16)] for h in range(2)]
-        g_word = [[keep.tile([P, 2 * HALF], U8, name=f"g_word{h}{g}", align_bytes=64) for g in range(PASSES)] for h in range(2)]
-        g_scale = [[keep.tile([P, HALF], U8, name=f"g_scale{h}{g}", align_bytes=64) for g in range(PASSES)] for h in range(2)]
+        g_word = [[keep.tile([P, 2 * HALF], U8, name=f"g_word0{g}", align_bytes=64) for g in range(PASSES)]]
+        g_word.append(
+            [
+                keep.tile([P, 2 * HALF], U8, name="g_word10", align_bytes=64),
+                reuse.tile([P, 2 * HALF], U8, name="g_word11", offset=8 * R, align_bytes=64),
+            ]
+        )
+        g_scale = [[keep.tile([P, HALF], U8, name=f"g_scale0{g}", align_bytes=64) for g in range(PASSES)]]
+        g_scale.append(
+            [reuse.tile([P, HALF], U8, name=f"g_scale1{g}", offset=8 * R + (2 + g) * HALF, align_bytes=64) for g in range(PASSES)]
+        )
 
         def gather_words(h):
             for g in range(PASSES):
@@ -88,8 +95,8 @@ def tile_moe_expert_hidden_over_peak_pl_kernel(
         wa_scale = keep.tile([P, PASSES, R], U8, name="wa_scale", align_bytes=64)
         gather_words(0)
         deal(nc, wa_word[:], wa_raw[:], 4)
-        deal(nc, wa_scale[:], wa_scale_raw[:], 16)
         gather_scales(0)
+        deal(nc, wa_scale[:], wa_scale_raw[:], 16)
         gather_words(1)
         gather_scales(1)
 
@@ -121,8 +128,11 @@ def tile_moe_expert_hidden_over_peak_pl_kernel(
             nc.scalar.activation(size[0][:, :, c * BLOCK : (c + 1) * BLOCK], z[c][:], ACT.Abs)
         for i in (1, 2):
             nc.scalar.activation(size[i][:], z[i + 1][:], ACT.Abs)
-        z_last = keep.tile([P, BLOCK, PACK], F32, name="z_last")
-        nc.scalar.copy(z_last[:], z[3][:].rearrange("p t j -> p j t"))
+
+        wb_word = keep.tile([P, 1, 2 * N], U8, name="wb_word", align_bytes=64)
+        wb_scale = keep.tile([P, 1, N], U8, name="wb_scale", align_bytes=64)
+        deal(nc, wb_scale[:], wb_scale_raw[:], 16)
+        deal(nc, wb_word[:].bitcast(U16), wb_raw[:].bitcast(U16), 8)
 
         divisor = None
         for i in range(3):
@@ -134,39 +144,26 @@ def tile_moe_expert_hidden_over_peak_pl_kernel(
             else:
                 nc.vector.scalar_tensor_tensor(running[:], peak[:], 0.1, divisor[:], ALU.add, ALU.max)
             divisor = running
-        wb_word = keep.tile([P, 1, 2 * N], U8, name="wb_word", tag="size2", align_bytes=64)
-        deal(nc, wb_word[:].bitcast(U16), wb_raw[:].bitcast(U16), 8)
         inverse = keep.tile([P, PACK], F32, name="inverse")
         nc.vector.reciprocal(inverse[:], divisor[:])
-        wb_scale = keep.tile([P, 1, N], U8, name="wb_scale", tag="running2", align_bytes=64)
-        deal(nc, wb_scale[:], wb_scale_raw[:], 16)
         gain = keep.tile([P, PACK], F32, name="gain")
         nc.vector.tensor_tensor(gain[:], inverse[:], factor[:], ALU.mult)
 
         hid = [keep.tile([P, HALF, PACK], BF16, name=f"hid{h}", align_bytes=64) for h in range(2)]
         h_word = [keep.tile([P, HALF], U32, name=f"h_word{h}", tag=f"h_word{h}", align_bytes=64) for h in range(2)]
-        h_scale = [keep.tile([P, HALF], U8, name=f"h_scale{h}", align_bytes=64) for h in range(2)]
+        h_scale = [keep.tile([P, HALF], U8, name=f"h_scale{h}", tag=f"h_scale{h}", align_bytes=64) for h in range(2)]
         p_bank = [[psum.tile([P, 2, HALF], F32, name=f"p_bank{h}{u}") for u in range(2)] for h in range(2)]
-        p_sb = [keep.tile([P, J], F32, name=f"p_sb{t}") for t in range(PACK)]
-        fifth = []
-
-        def scale_stream(t, tag, align):
-            part = keep.tile([P, T], F32, name=f"fifth{t}", tag=tag, align_bytes=align)
-            nc.scalar.mul(part[:], stream[:, t, :], 0.2)
-            fifth.append(part[:])
-
-        scale_stream(0, "size1", 64)
-        scale_stream(1, "peak2", 64)
+        p_sb = [keep.tile([P, J], F32, name=f"p_sb{t}", tag=f"p_sb{t}", align_bytes=64) for t in range(PACK)]
         spread = gain[:].unsqueeze(1).to_broadcast([P, BLOCK, PACK])
-        nc.gpsimd.tensor_tensor(hid[1][:, BLOCK:HALF, :], z_last[:], spread, ALU.mult)
-        for b in range(3):
+
+        def normalise(b):
             h, c = divmod(b, 2)
             nc.vector.tensor_tensor(hid[h][:, c * BLOCK : (c + 1) * BLOCK, :], z[b][:].rearrange("p t j -> p j t"), spread, ALU.mult)
-        for h in range(2):
+
+        def second_product(h):
             nc.vector.quantize_mx(
                 out=h_word[h][:].bitcast(FP8X4), scales=h_scale[h][:], in_=hid[h][:].rearrange("p j t -> p (j t)")
             )
-            cols = slice(h * HALF, (h + 1) * HALF)
             for t in range(PACK):
                 nc.tensor.matmul_mx(
                     out=p_bank[h][t // 2][:, t % 2, :],
@@ -177,12 +174,29 @@ def tile_moe_expert_hidden_over_peak_pl_kernel(
                     start=True,
                     stop=True,
                 )
-            for t in range(2):
-                nc.scalar.copy(p_sb[t][:, cols], p_bank[h][0][:, t, :])
-        for h in range(2):
-            for t in range(2, PACK):
-                nc.scalar.copy(p_sb[t][:, h * HALF : (h + 1) * HALF], p_bank[h][1][:, t % 2, :])
-        scale_stream(2, "h_word1", 64)
+
+        def empty_bank(h, u):
+            for e in range(2):
+                nc.scalar.copy(p_sb[2 * u + e][:, h * HALF : (h + 1) * HALF], p_bank[h][u][:, e, :])
+
+        fifth = []
+
+        def scale_stream(t, tag):
+            part = keep.tile([P, T], F32, name=f"fifth{t}", tag=tag, align_bytes=64)
+            nc.scalar.mul(part[:], stream[:, t, :], 0.2)
+            fifth.append(part[:])
+
+        for b in range(3):
+            normalise(b)
+        second_product(0)
+        normalise(3)
+        second_product(1)
+        empty_bank(0, 0)
+        empty_bank(1, 0)
+        scale_stream(0, "h_word1")
+        empty_bank(0, 1)
+        empty_bank(1, 1)
+        scale_stream(1, "h_scale1")
 
         y = [[keep.tile([P, 2, COLS], F32, name=f"y{u}{k}") for k in range(2)] for u in range(2)]
         y_round = [keep.tile([P, COLS, PACK], BF16, name=f"y_round{k}", align_bytes=64) for k in range(2)]
@@ -207,6 +221,7 @@ def tile_moe_expert_hidden_over_peak_pl_kernel(
             if t == 0:
                 for h in range(2):
                     nc.vector.tensor_copy(placed[t][:].indirect(lists[h]), p_sb[t][:, h * HALF : (h + 1) * HALF])
+                scale_stream(2, "p_sb0")
             else:
                 nc.vector.tensor_copy(placed[t][:].indirect(offsets[:]), p_sb[t][:])
             for k in range(2):

@@ -23,9 +23,14 @@ PASSES = K // (P * PACK)
 HALF = J // 2
 BLOCK = 128
 COLS = T // 2
+LINE = 16
+ALIGN = 64
+PEAK_OFFSET = 0.1
+STREAM_WEIGHT = 0.2
 
 
-def deal(nc, dst, src, run):
+def deal(nc, dst, src, element_bytes):
+    run = LINE // element_bytes
     nc.vector.tensor_copy(
         out=dst.rearrange("p g (t b i) -> p g b t i", t=PACK, i=run),
         in_=src.rearrange("p g (b i t) -> p g b t i", t=PACK, i=run),
@@ -46,20 +51,22 @@ def tile_moe_expert_hidden_over_peak_pl_kernel(
         keep = ctx.enter_context(tc.tile_pool(name="keep", bufs=1))
         reuse = ctx.enter_context(tc.tile_pool(name="reuse", bufs=1))
         psum = ctx.enter_context(tc.psum_pool(name="psum", bufs=1))
+        wa_raw_at = 0
+        wa_scale_raw_at = wa_raw_at + PASSES * R * 4
 
         offsets = keep.tile([P, J // 16], U16, name="offsets")
         nc.sync.dma_start(offsets[:], offs)
 
-        x_scale = keep.tile([P, PASSES, T], U8, name="x_scale", align_bytes=64)
-        wa_scale_raw = reuse.tile([P, PASSES, R], U8, name="wa_scale_raw", offset=8 * R)
-        wb_scale_raw = keep.tile([P, 1, N], U8, name="wb_scale_raw", align_bytes=64)
+        x_scale = keep.tile([P, PASSES, T], U8, name="x_scale", align_bytes=ALIGN)
+        wa_scale_raw = reuse.tile([P, PASSES, R], U8, name="wa_scale_raw", offset=wa_scale_raw_at)
+        wb_scale_raw = keep.tile([P, 1, N], U8, name="wb_scale_raw", align_bytes=ALIGN)
         for plane in (x_scale, wa_scale_raw, wb_scale_raw):
             nc.vector.memset(plane[:].bitcast(I32), 0)
 
-        x_word = [keep.tile([P, 2 * T], U8, name=f"x_word{g}", tag=f"x_word{g}", align_bytes=64) for g in range(PASSES)]
+        x_word = [keep.tile([P, 2 * T], U8, name=f"x_word{g}", tag=f"x_word{g}", align_bytes=ALIGN) for g in range(PASSES)]
         for g in range(PASSES):
             nc.sync.dma_start(out=x_word[g][:].bitcast(I32), in_=xt_words[g].bitcast(I32))
-        wa_raw = reuse.tile([P, PASSES, R], I32, name="wa_raw", offset=0)
+        wa_raw = reuse.tile([P, PASSES, R], I32, name="wa_raw", offset=wa_raw_at)
         nc.sync.dma_start(out=wa_raw[:], in_=wa_words.rearrange("g p c r -> p g (c r)").bitcast(I32))
         load_scale_rows(nc.scalar, x_scale, xt_scales)
         load_scale_rows(nc.sync, wa_scale_raw, wa_scales)
@@ -71,16 +78,19 @@ def tile_moe_expert_hidden_over_peak_pl_kernel(
         placed = [windows[t % 2] for t in range(PACK)]
 
         lists = [offsets[:, h * (HALF // 16) : (h + 1) * (HALF // 16)] for h in range(2)]
-        g_word = [[keep.tile([P, 2 * HALF], U8, name=f"g_word0{g}", align_bytes=64) for g in range(PASSES)]]
+        g_word = [[keep.tile([P, 2 * HALF], U8, name=f"g_word0{g}", align_bytes=ALIGN) for g in range(PASSES)]]
         g_word.append(
             [
-                keep.tile([P, 2 * HALF], U8, name="g_word10", align_bytes=64),
-                reuse.tile([P, 2 * HALF], U8, name="g_word11", offset=8 * R, align_bytes=64),
+                keep.tile([P, 2 * HALF], U8, name="g_word10", align_bytes=ALIGN),
+                reuse.tile([P, 2 * HALF], U8, name="g_word11", offset=wa_scale_raw_at, align_bytes=ALIGN),
             ]
         )
-        g_scale = [[keep.tile([P, HALF], U8, name=f"g_scale0{g}", align_bytes=64) for g in range(PASSES)]]
+        g_scale = [[keep.tile([P, HALF], U8, name=f"g_scale0{g}", align_bytes=ALIGN) for g in range(PASSES)]]
         g_scale.append(
-            [reuse.tile([P, HALF], U8, name=f"g_scale1{g}", offset=8 * R + (2 + g) * HALF, align_bytes=64) for g in range(PASSES)]
+            [
+                reuse.tile([P, HALF], U8, name=f"g_scale1{g}", offset=wa_scale_raw_at + (2 + g) * HALF, align_bytes=ALIGN)
+                for g in range(PASSES)
+            ]
         )
 
         def gather_words(h):
@@ -91,24 +101,24 @@ def tile_moe_expert_hidden_over_peak_pl_kernel(
             for g in range(PASSES):
                 nc.vector.tensor_copy(g_scale[h][g][:], x_scale[:, g, :].indirect(lists[h]))
 
-        wa_word = keep.tile([P, PASSES, R], I32, name="wa_word", align_bytes=64)
-        wa_scale = keep.tile([P, PASSES, R], U8, name="wa_scale", align_bytes=64)
+        wa_word = keep.tile([P, PASSES, R], I32, name="wa_word", align_bytes=ALIGN)
+        wa_scale = keep.tile([P, PASSES, R], U8, name="wa_scale", align_bytes=ALIGN)
         gather_words(0)
         deal(nc, wa_word[:], wa_raw[:], 4)
         gather_scales(0)
-        deal(nc, wa_scale[:], wa_scale_raw[:], 16)
+        deal(nc, wa_scale[:], wa_scale_raw[:], 1)
         gather_words(1)
         gather_scales(1)
 
-        wb_raw = reuse.tile([P, 1, 2 * N], U8, name="wb_raw", offset=0)
+        wb_raw = reuse.tile([P, 1, 2 * N], U8, name="wb_raw", offset=wa_raw_at)
         nc.sync.dma_start(out=wb_raw[:].bitcast(I32), in_=wb_words.rearrange("g p c -> p g c").bitcast(I32))
-        factor = reuse.tile([P, PACK], F32, name="factor", offset=3 * N)
+        factor = reuse.tile([P, PACK], F32, name="factor", offset=wa_raw_at + 3 * N)
         nc.sync.dma_start(out=factor[:], in_=us.rearrange("(p t) o -> p (t o)", t=PACK))
-        stream = keep.tile([P, PACK, T], F32, name="stream", tag="x_word0", align_bytes=64)
+        stream = keep.tile([P, PACK, T], F32, name="stream", tag="x_word0", align_bytes=ALIGN)
         nc.sync.dma_start(out=stream[:], in_=res.rearrange("(p t) c -> p t c", t=PACK))
 
-        z = [psum.tile([P, PACK, BLOCK], F32, name=f"z{b}") for b in range(4)]
-        for b in range(4):
+        z = [psum.tile([P, PACK, BLOCK], F32, name=f"z{b}") for b in range(J // BLOCK)]
+        for b in range(J // BLOCK):
             h, c = divmod(b, 2)
             for t in range(PACK):
                 for g in range(PASSES):
@@ -123,50 +133,53 @@ def tile_moe_expert_hidden_over_peak_pl_kernel(
                     )
 
         widths = (HALF, BLOCK, BLOCK)
-        size = [keep.tile([P, PACK, w], F32, name=f"size{i}", tag=f"size{i}", align_bytes=64) for i, w in enumerate(widths)]
+        size = [keep.tile([P, PACK, w], F32, name=f"size{i}", tag=f"size{i}", align_bytes=ALIGN) for i, w in enumerate(widths)]
         for c in range(2):
             nc.scalar.activation(size[0][:, :, c * BLOCK : (c + 1) * BLOCK], z[c][:], ACT.Abs)
         for i in (1, 2):
             nc.scalar.activation(size[i][:], z[i + 1][:], ACT.Abs)
 
-        wb_word = keep.tile([P, 1, 2 * N], U8, name="wb_word", align_bytes=64)
-        wb_scale = keep.tile([P, 1, N], U8, name="wb_scale", align_bytes=64)
-        deal(nc, wb_scale[:], wb_scale_raw[:], 16)
-        deal(nc, wb_word[:].bitcast(U16), wb_raw[:].bitcast(U16), 8)
+        wb_word = keep.tile([P, 1, 2 * N], U8, name="wb_word", align_bytes=ALIGN)
+        wb_scale = keep.tile([P, 1, N], U8, name="wb_scale", align_bytes=ALIGN)
+        deal(nc, wb_scale[:], wb_scale_raw[:], 1)
+        deal(nc, wb_word[:].bitcast(U16), wb_raw[:].bitcast(U16), 2)
 
         divisor = None
-        for i in range(3):
-            peak = keep.tile([P, PACK], F32, name=f"peak{i}", tag=f"peak{i}", align_bytes=64)
+        for i in range(len(widths)):
+            peak = keep.tile([P, PACK], F32, name=f"peak{i}", tag=f"peak{i}", align_bytes=ALIGN)
             nc.vector.tensor_reduce(peak[:], size[i][:], AXIS.X, ALU.max)
-            running = keep.tile([P, PACK], F32, name=f"running{i}", tag=f"running{i}", align_bytes=64)
+            running = keep.tile([P, PACK], F32, name=f"running{i}", tag=f"running{i}", align_bytes=ALIGN)
             if i == 0:
-                nc.vector.tensor_scalar(running[:], peak[:], 0.1, None, ALU.add)
+                nc.vector.tensor_scalar(running[:], peak[:], PEAK_OFFSET, None, ALU.add)
             else:
-                nc.vector.scalar_tensor_tensor(running[:], peak[:], 0.1, divisor[:], ALU.add, ALU.max)
+                nc.vector.scalar_tensor_tensor(running[:], peak[:], PEAK_OFFSET, divisor[:], ALU.add, ALU.max)
             divisor = running
         inverse = keep.tile([P, PACK], F32, name="inverse")
         nc.vector.reciprocal(inverse[:], divisor[:])
         gain = keep.tile([P, PACK], F32, name="gain")
         nc.vector.tensor_tensor(gain[:], inverse[:], factor[:], ALU.mult)
 
-        hid = [keep.tile([P, HALF, PACK], BF16, name=f"hid{h}", align_bytes=64) for h in range(2)]
-        h_word = [keep.tile([P, HALF], U32, name=f"h_word{h}", tag=f"h_word{h}", align_bytes=64) for h in range(2)]
-        h_scale = [keep.tile([P, HALF], U8, name=f"h_scale{h}", tag=f"h_scale{h}", align_bytes=64) for h in range(2)]
-        p_bank = [[psum.tile([P, 2, HALF], F32, name=f"p_bank{h}{u}") for u in range(2)] for h in range(2)]
-        p_sb = [keep.tile([P, J], F32, name=f"p_sb{t}", tag=f"p_sb{t}", align_bytes=64) for t in range(PACK)]
+        hid = [keep.tile([P, HALF, PACK], BF16, name=f"hid{h}", align_bytes=ALIGN) for h in range(2)]
+        h_word = [keep.tile([P, HALF], U32, name=f"h_word{h}", tag=f"h_word{h}", align_bytes=ALIGN) for h in range(2)]
+        h_scale = [keep.tile([P, HALF], U8, name=f"h_scale{h}", tag=f"h_scale{h}", align_bytes=ALIGN) for h in range(2)]
+        p_bank = [[psum.tile([P, 2, HALF], F32, name=f"p_bank{h}{e}") for e in range(2)] for h in range(2)]
+        p_sb = [keep.tile([P, J], F32, name=f"p_sb{t}", tag=f"p_sb{t}", align_bytes=ALIGN) for t in range(PACK)]
         spread = gain[:].unsqueeze(1).to_broadcast([P, BLOCK, PACK])
 
         def normalise(b):
             h, c = divmod(b, 2)
             nc.vector.tensor_tensor(hid[h][:, c * BLOCK : (c + 1) * BLOCK, :], z[b][:].rearrange("p t j -> p j t"), spread, ALU.mult)
 
-        def second_product(h):
+        def quantise_hid(h):
             nc.vector.quantize_mx(
                 out=h_word[h][:].bitcast(FP8X4), scales=h_scale[h][:], in_=hid[h][:].rearrange("p j t -> p (j t)")
             )
-            for t in range(PACK):
+
+        def second_product(h, u):
+            for e in range(2):
+                t = 2 * u + e
                 nc.tensor.matmul_mx(
-                    out=p_bank[h][t // 2][:, t % 2, :],
+                    out=p_bank[h][e][:, u, :],
                     lhsT=wb_word[:, 0, 2 * t * P : 2 * (t + 1) * P].bitcast(FP4X4),
                     lhsT_scale=wb_scale[:, 0, t * P : (t + 1) * P],
                     rhs=h_word[h][:].bitcast(FP8X4),
@@ -175,33 +188,39 @@ def tile_moe_expert_hidden_over_peak_pl_kernel(
                     stop=True,
                 )
 
-        def empty_bank(h, u):
+        def copy_out(h, u):
             for e in range(2):
-                nc.scalar.copy(p_sb[2 * u + e][:, h * HALF : (h + 1) * HALF], p_bank[h][u][:, e, :])
+                nc.scalar.copy(p_sb[2 * u + e][:, h * HALF : (h + 1) * HALF], p_bank[h][e][:, u, :])
 
-        fifth = []
+        weighted = []
 
-        def scale_stream(t, tag):
-            part = keep.tile([P, T], F32, name=f"fifth{t}", tag=tag, align_bytes=64)
-            nc.scalar.mul(part[:], stream[:, t, :], 0.2)
-            fifth.append(part[:])
+        def weigh_stream(t, tag):
+            part = keep.tile([P, T], F32, name=f"weighted{t}", tag=tag, align_bytes=ALIGN)
+            nc.scalar.mul(part[:], stream[:, t, :], STREAM_WEIGHT)
+            weighted.append(part[:])
 
-        for b in range(3):
-            normalise(b)
-        second_product(0)
-        normalise(3)
-        second_product(1)
-        empty_bank(0, 0)
-        empty_bank(1, 0)
-        scale_stream(0, "h_word1")
-        empty_bank(0, 1)
-        empty_bank(1, 1)
-        scale_stream(1, "h_scale1")
+        for t in range(PACK):
+            nc.scalar.activation(hid[1][:, BLOCK:HALF, t], z[3][:, t, :], ACT.Copy, scale=gain[:, t : t + 1])
+        normalise(0)
+        normalise(1)
+        quantise_hid(0)
+        normalise(2)
+        second_product(0, 0)
+        copy_out(0, 0)
+        quantise_hid(1)
+        second_product(1, 0)
+        copy_out(1, 0)
+        for h in range(2):
+            second_product(h, 1)
+        weigh_stream(0, "h_word1")
+        for h in range(2):
+            copy_out(h, 1)
+        weigh_stream(1, "h_scale1")
 
         y = [[keep.tile([P, 2, COLS], F32, name=f"y{u}{k}") for k in range(2)] for u in range(2)]
-        y_round = [keep.tile([P, COLS, PACK], BF16, name=f"y_round{k}", align_bytes=64) for k in range(2)]
-        y_word = [keep.tile([P, COLS], U32, name=f"y_word{k}", align_bytes=64) for k in range(2)]
-        y_scale = keep.tile([P, T], U8, name="y_scale", align_bytes=64)
+        y_round = [keep.tile([P, COLS, PACK], BF16, name=f"y_round{k}", align_bytes=ALIGN) for k in range(2)]
+        y_word = [keep.tile([P, COLS], U32, name=f"y_word{k}", align_bytes=ALIGN) for k in range(2)]
+        y_scale = keep.tile([P, T], U8, name="y_scale", align_bytes=ALIGN)
         out_rows = out_0.rearrange("(p t) c -> p t c", t=PACK)
         out_words = out_1[0].rearrange("p c r -> p (c r)").bitcast(I32)
 
@@ -209,9 +228,11 @@ def tile_moe_expert_hidden_over_peak_pl_kernel(
             u, e = divmod(t, 2)
             cols = slice(k * COLS, (k + 1) * COLS)
             if t < PACK - 1:
-                nc.gpsimd.tensor_tensor(y[u][k][:, e, :], fifth[t][:, cols], placed[t][:, cols], ALU.add)
+                nc.gpsimd.tensor_tensor(y[u][k][:, e, :], weighted[t][:, cols], placed[t][:, cols], ALU.add)
             else:
-                nc.vector.scalar_tensor_tensor(y[u][k][:, e, :], stream[:, t, cols], 0.2, placed[t][:, cols], ALU.mult, ALU.add)
+                nc.vector.scalar_tensor_tensor(
+                    y[u][k][:, e, :], stream[:, t, cols], STREAM_WEIGHT, placed[t][:, cols], ALU.mult, ALU.add
+                )
             nc.sync.dma_start(out=out_rows[:, t, cols], in_=y[u][k][:, e, :])
 
         def round_pair(copy, u, k, cols):
@@ -221,7 +242,7 @@ def tile_moe_expert_hidden_over_peak_pl_kernel(
             if t == 0:
                 for h in range(2):
                     nc.vector.tensor_copy(placed[t][:].indirect(lists[h]), p_sb[t][:, h * HALF : (h + 1) * HALF])
-                scale_stream(2, "p_sb0")
+                weigh_stream(2, "p_sb0")
             else:
                 nc.vector.tensor_copy(placed[t][:].indirect(offsets[:]), p_sb[t][:])
             for k in range(2):

from contextlib import ExitStack

import concourse.mybir as mybir

K, T, J, R, N = 1024, 1024, 512, 512, 512
FLOPS = 2 * K * R * J + 2 * R * N * J

F32 = mybir.dt.float32
BF16 = mybir.dt.bfloat16
I32 = mybir.dt.int32
U32 = mybir.dt.uint32
U16 = mybir.dt.uint16
U8 = mybir.dt.uint8
FP8X4 = mybir.dt.float8_e4m3fn_x4
FP4X4 = mybir.dt.float4_e2m1fn_x4
ALU = mybir.AluOpType
ACT = mybir.ActivationFunctionType
AXIS = mybir.AxisListType

P = 128
PACK = 4
PASSES = K // (P * PACK)
HALF = J // 2
BLOCK = 128
COLS = T // 2
LINE = 16
ALIGN = 64
PEAK_OFFSET = 0.1
STREAM_WEIGHT = 0.2


def deal(nc, dst, src, element_bytes):
    run = LINE // element_bytes
    nc.vector.tensor_copy(
        out=dst.rearrange("p g (t b i) -> p g b t i", t=PACK, i=run),
        in_=src.rearrange("p g (b i t) -> p g b t i", t=PACK, i=run),
    )


def load_scale_rows(queue, plane, scales):
    rows = scales.rearrange("g (Q q) c -> q Q g c", q=4)
    for q in range(4):
        queue.dma_start(out=plane[q:P:32].bitcast(I32), in_=rows[q].bitcast(I32))


def tile_moe_expert_hidden_over_peak_pl_kernel(
    tc, xt_words, xt_scales, wa_words, wa_scales, us, wb_words, wb_scales, res, offs, out_0, out_1, out_2
):
    nc = tc.nc
    with ExitStack() as ctx:
        keep = ctx.enter_context(tc.tile_pool(name="keep", bufs=1))
        reuse = ctx.enter_context(tc.tile_pool(name="reuse", bufs=1))
        psum = ctx.enter_context(tc.psum_pool(name="psum", bufs=1))
        wa_raw_at = 0
        wa_scale_raw_at = wa_raw_at + PASSES * R * 4

        offsets = keep.tile([P, J // 16], U16, name="offsets")
        nc.sync.dma_start(offsets[:], offs)

        x_scale = keep.tile([P, PASSES, T], U8, name="x_scale", align_bytes=ALIGN)
        wa_scale_raw = reuse.tile([P, PASSES, R], U8, name="wa_scale_raw", offset=wa_scale_raw_at)
        wb_scale_raw = keep.tile([P, 1, N], U8, name="wb_scale_raw", align_bytes=ALIGN)
        for plane in (x_scale, wa_scale_raw, wb_scale_raw):
            nc.vector.memset(plane[:].bitcast(I32), 0)

        x_word = [keep.tile([P, 2 * T], U8, name=f"x_word{g}", tag=f"x_word{g}", align_bytes=ALIGN) for g in range(PASSES)]
        for g in range(PASSES):
            nc.sync.dma_start(out=x_word[g][:].bitcast(I32), in_=xt_words[g].bitcast(I32))
        wa_raw = reuse.tile([P, PASSES, R], I32, name="wa_raw", offset=wa_raw_at)
        nc.sync.dma_start(out=wa_raw[:], in_=wa_words.rearrange("g p c r -> p g (c r)").bitcast(I32))
        load_scale_rows(nc.scalar, x_scale, xt_scales)
        load_scale_rows(nc.sync, wa_scale_raw, wa_scales)
        load_scale_rows(nc.sync, wb_scale_raw, wb_scales)

        windows = [keep.tile([P, T], F32, name=f"window{w}") for w in range(2)]
        for w in range(2):
            nc.vector.memset(windows[w][:], 0.0)
        placed = [windows[t % 2] for t in range(PACK)]

        lists = [offsets[:, h * (HALF // 16) : (h + 1) * (HALF // 16)] for h in range(2)]
        g_word = [[keep.tile([P, 2 * HALF], U8, name=f"g_word0{g}", align_bytes=ALIGN) for g in range(PASSES)]]
        g_word.append(
            [
                keep.tile([P, 2 * HALF], U8, name="g_word10", align_bytes=ALIGN),
                reuse.tile([P, 2 * HALF], U8, name="g_word11", offset=wa_scale_raw_at, align_bytes=ALIGN),
            ]
        )
        g_scale = [[keep.tile([P, HALF], U8, name=f"g_scale0{g}", align_bytes=ALIGN) for g in range(PASSES)]]
        g_scale.append(
            [
                reuse.tile([P, HALF], U8, name=f"g_scale1{g}", offset=wa_scale_raw_at + (2 + g) * HALF, align_bytes=ALIGN)
                for g in range(PASSES)
            ]
        )

        def gather_words(h):
            for g in range(PASSES):
                nc.vector.tensor_copy(g_word[h][g][:].bitcast(U16), x_word[g][:].bitcast(U16).indirect(lists[h]))

        def gather_scales(h):
            for g in range(PASSES):
                nc.vector.tensor_copy(g_scale[h][g][:], x_scale[:, g, :].indirect(lists[h]))

        wa_word = keep.tile([P, PASSES, R], I32, name="wa_word", align_bytes=ALIGN)
        wa_scale = keep.tile([P, PASSES, R], U8, name="wa_scale", align_bytes=ALIGN)
        gather_words(0)
        deal(nc, wa_word[:], wa_raw[:], 4)
        gather_scales(0)
        deal(nc, wa_scale[:], wa_scale_raw[:], 1)
        gather_words(1)
        gather_scales(1)

        wb_raw = reuse.tile([P, 1, 2 * N], U8, name="wb_raw", offset=wa_raw_at)
        nc.sync.dma_start(out=wb_raw[:].bitcast(I32), in_=wb_words.rearrange("g p c -> p g c").bitcast(I32))
        factor = reuse.tile([P, PACK], F32, name="factor", offset=wa_raw_at + 3 * N)
        nc.sync.dma_start(out=factor[:], in_=us.rearrange("(p t) o -> p (t o)", t=PACK))
        stream = keep.tile([P, PACK, T], F32, name="stream", tag="x_word0", align_bytes=ALIGN)
        nc.sync.dma_start(out=stream[:], in_=res.rearrange("(p t) c -> p t c", t=PACK))

        z = [psum.tile([P, PACK, BLOCK], F32, name=f"z{b}") for b in range(J // BLOCK)]
        for b in range(J // BLOCK):
            h, c = divmod(b, 2)
            for t in range(PACK):
                for g in range(PASSES):
                    nc.tensor.matmul_mx(
                        out=z[b][:, t, :],
                        lhsT=wa_word[:, g, t * P : (t + 1) * P].bitcast(FP8X4),
                        lhsT_scale=wa_scale[:, g, t * P : (t + 1) * P],
                        rhs=g_word[h][g][:, 2 * c * BLOCK : 2 * (c + 1) * BLOCK].bitcast(FP4X4),
                        rhs_scale=g_scale[h][g][:, c * BLOCK : (c + 1) * BLOCK],
                        start=(g == 0),
                        stop=(g == PASSES - 1),
                    )

        widths = (HALF, BLOCK, BLOCK)
        size = [keep.tile([P, PACK, w], F32, name=f"size{i}", tag=f"size{i}", align_bytes=ALIGN) for i, w in enumerate(widths)]
        for c in range(2):
            nc.scalar.activation(size[0][:, :, c * BLOCK : (c + 1) * BLOCK], z[c][:], ACT.Abs)
        for i in (1, 2):
            nc.scalar.activation(size[i][:], z[i + 1][:], ACT.Abs)

        wb_word = keep.tile([P, 1, 2 * N], U8, name="wb_word", align_bytes=ALIGN)
        wb_scale = keep.tile([P, 1, N], U8, name="wb_scale", align_bytes=ALIGN)
        deal(nc, wb_scale[:], wb_scale_raw[:], 1)
        deal(nc, wb_word[:].bitcast(U16), wb_raw[:].bitcast(U16), 2)

        divisor = None
        for i in range(len(widths)):
            peak = keep.tile([P, PACK], F32, name=f"peak{i}", tag=f"peak{i}", align_bytes=ALIGN)
            nc.vector.tensor_reduce(peak[:], size[i][:], AXIS.X, ALU.max)
            running = keep.tile([P, PACK], F32, name=f"running{i}", tag=f"running{i}", align_bytes=ALIGN)
            if i == 0:
                nc.vector.tensor_scalar(running[:], peak[:], PEAK_OFFSET, None, ALU.add)
            else:
                nc.vector.scalar_tensor_tensor(running[:], peak[:], PEAK_OFFSET, divisor[:], ALU.add, ALU.max)
            divisor = running
        inverse = keep.tile([P, PACK], F32, name="inverse")
        nc.vector.reciprocal(inverse[:], divisor[:])
        gain = keep.tile([P, PACK], F32, name="gain")
        nc.vector.tensor_tensor(gain[:], inverse[:], factor[:], ALU.mult)

        hid = [keep.tile([P, HALF, PACK], BF16, name=f"hid{h}", align_bytes=ALIGN) for h in range(2)]
        h_word = [keep.tile([P, HALF], U32, name=f"h_word{h}", tag=f"h_word{h}", align_bytes=ALIGN) for h in range(2)]
        h_scale = [keep.tile([P, HALF], U8, name=f"h_scale{h}", tag=f"h_scale{h}", align_bytes=ALIGN) for h in range(2)]
        p_bank = [[psum.tile([P, 2, HALF], F32, name=f"p_bank{h}{e}") for e in range(2)] for h in range(2)]
        p_sb = [keep.tile([P, J], F32, name=f"p_sb{t}", tag=f"p_sb{t}", align_bytes=ALIGN) for t in range(PACK)]
        spread = gain[:].unsqueeze(1).to_broadcast([P, BLOCK, PACK])

        def normalise(b):
            h, c = divmod(b, 2)
            nc.vector.tensor_tensor(hid[h][:, c * BLOCK : (c + 1) * BLOCK, :], z[b][:].rearrange("p t j -> p j t"), spread, ALU.mult)

        def quantise_hid(h):
            nc.vector.quantize_mx(
                out=h_word[h][:].bitcast(FP8X4), scales=h_scale[h][:], in_=hid[h][:].rearrange("p j t -> p (j t)")
            )

        def second_product(h, u):
            for e in range(2):
                t = 2 * u + e
                nc.tensor.matmul_mx(
                    out=p_bank[h][e][:, u, :],
                    lhsT=wb_word[:, 0, 2 * t * P : 2 * (t + 1) * P].bitcast(FP4X4),
                    lhsT_scale=wb_scale[:, 0, t * P : (t + 1) * P],
                    rhs=h_word[h][:].bitcast(FP8X4),
                    rhs_scale=h_scale[h][:],
                    start=True,
                    stop=True,
                )

        def copy_out(h, u):
            for e in range(2):
                nc.scalar.copy(p_sb[2 * u + e][:, h * HALF : (h + 1) * HALF], p_bank[h][e][:, u, :])

        weighted = []

        def weigh_stream(t, tag):
            part = keep.tile([P, T], F32, name=f"weighted{t}", tag=tag, align_bytes=ALIGN)
            nc.scalar.mul(part[:], stream[:, t, :], STREAM_WEIGHT)
            weighted.append(part[:])

        for t in range(PACK):
            nc.scalar.activation(hid[1][:, BLOCK:HALF, t], z[3][:, t, :], ACT.Copy, scale=gain[:, t : t + 1])
        normalise(0)
        normalise(1)
        quantise_hid(0)
        normalise(2)
        second_product(0, 0)
        copy_out(0, 0)
        quantise_hid(1)
        second_product(1, 0)
        copy_out(1, 0)
        for h in range(2):
            second_product(h, 1)
        weigh_stream(0, "h_word1")
        for h in range(2):
            copy_out(h, 1)
        weigh_stream(1, "h_scale1")

        y = [[keep.tile([P, 2, COLS], F32, name=f"y{u}{k}") for k in range(2)] for u in range(2)]
        y_round = [keep.tile([P, COLS, PACK], BF16, name=f"y_round{k}", align_bytes=ALIGN) for k in range(2)]
        y_word = [keep.tile([P, COLS], U32, name=f"y_word{k}", align_bytes=ALIGN) for k in range(2)]
        y_scale = keep.tile([P, T], U8, name="y_scale", align_bytes=ALIGN)
        out_rows = out_0.rearrange("(p t) c -> p t c", t=PACK)
        out_words = out_1[0].rearrange("p c r -> p (c r)").bitcast(I32)

        def add_stream(t, k):
            u, e = divmod(t, 2)
            cols = slice(k * COLS, (k + 1) * COLS)
            if t < PACK - 1:
                nc.gpsimd.tensor_tensor(y[u][k][:, e, :], weighted[t][:, cols], placed[t][:, cols], ALU.add)
            else:
                nc.vector.scalar_tensor_tensor(
                    y[u][k][:, e, :], stream[:, t, cols], STREAM_WEIGHT, placed[t][:, cols], ALU.mult, ALU.add
                )
            nc.sync.dma_start(out=out_rows[:, t, cols], in_=y[u][k][:, e, :])

        def round_pair(copy, u, k, cols):
            copy(y_round[k][:, cols, 2 * u : 2 * u + 2], y[u][k][:, :, cols].rearrange("p e c -> p c e"))

        for t in range(PACK):
            if t == 0:
                for h in range(2):
                    nc.vector.tensor_copy(placed[t][:].indirect(lists[h]), p_sb[t][:, h * HALF : (h + 1) * HALF])
                weigh_stream(2, "p_sb0")
            else:
                nc.vector.tensor_copy(placed[t][:].indirect(offsets[:]), p_sb[t][:])
            for k in range(2):
                add_stream(t, k)
                if t == 1:
                    round_pair(nc.scalar.copy, 0, k, slice(0, COLS))
        for k in range(2):
            round_pair(nc.scalar.copy, 1, k, slice(0, COLS // 2))
        for k in range(2):
            round_pair(nc.vector.tensor_copy, 1, k, slice(COLS // 2, COLS))
        for k in range(2):
            nc.vector.quantize_mx(
                out=y_word[k][:].bitcast(FP8X4),
                scales=y_scale[:, k * COLS : (k + 1) * COLS],
                in_=y_round[k][:].rearrange("p c t -> p (c t)"),
            )
            nc.sync.dma_start(out=out_words[:, k * COLS : (k + 1) * COLS], in_=y_word[k][:].bitcast(I32))
        out_scale_rows = out_2[0].rearrange("(Q q) c -> q Q c", q=4)
        for q in range(4):
            queue = nc.scalar if q < 2 else nc.sync
            queue.dma_start(out=out_scale_rows[q].bitcast(I32), in_=y_scale[q:P:32].bitcast(I32))
